import numpy as np
import ml_dtypes


def mxq(x, axis, fmt="e4m3"):
    dtype, down = {"e4m3": (ml_dtypes.float8_e4m3fn, 7), "e5m2": (ml_dtypes.float8_e5m2, 14)}[fmt]
    v = np.moveaxis(np.asarray(x, np.float32).astype(ml_dtypes.bfloat16).astype(np.float64), axis, -1)
    blocks = v.reshape(v.shape[:-1] + (-1, 32))
    amax = np.abs(blocks).max(-1, keepdims=True)
    byte = np.maximum(np.where(amax > 0, np.frexp(amax)[1] - 1 + 127, 0) - down, 1)
    scale = np.exp2(byte - 127.0)
    codes = (blocks / scale).astype(np.float32).astype(dtype).astype(np.float64)
    return np.moveaxis((codes * scale).reshape(v.shape), -1, axis)


WIDE = False


def mx_kscale(k):
    if not WIDE:
        return np.ones(k)
    levels = np.array([10, -10, 5, -5, 0])
    if k % 512:
        return np.exp2(np.random.permutation(np.resize(levels, k // 32))).repeat(32)
    a = np.empty((k // 512, 16))
    for p in range(k // 512):
        a[p, :8] = np.random.permutation(np.resize(levels, 8))
        for g in range(8):
            far = levels[np.abs(levels - a[p, g]) >= 10]
            a[p, g + 8] = far[np.random.randint(len(far))]
    return np.exp2(a.ravel()).repeat(32)


def f64(x):
    return np.asarray(x).astype(np.float64)


def striped(idx):
    return np.tile(idx.reshape(-1, 16).T, (8, 1)).astype(np.uint16)


def unstriped(offs):
    return offs[:16].T.reshape(-1).astype(np.int64)


E2M1 = np.array([0.0, 0.5, 1.0, 1.5, 2.0, 3.0, 4.0, 6.0, -0.0, -0.5, -1.0, -1.5, -2.0, -3.0, -4.0, -6.0])


def pack_weight(w, fmt):
    k, n = w.shape
    w = f64(np.asarray(w, np.float32).astype(ml_dtypes.bfloat16)).reshape(k // 32, 32, n)
    amax = np.abs(w).max(1)
    if fmt == "e4m3":
        byte = np.frexp(amax)[1] - 1 + 127 - 7
    else:
        mant, ex = np.frexp(amax / 6.0)
        byte = np.where(mant > 0.5, ex, ex - 1) + 127
    byte = np.clip(np.where(amax > 0, byte, 1), 1, 254)
    scaled = (w * np.exp2(127.0 - byte)[:, None, :]).reshape(k, n).astype(np.float32)
    by_word = np.ascontiguousarray(scaled.reshape(k // 512, 128, 4, n).transpose(0, 1, 3, 2))
    if fmt == "e4m3":
        words = by_word.astype(ml_dtypes.float8_e4m3fn).view(np.uint8)
    else:
        c = by_word.astype(ml_dtypes.float4_e2m1fn).view(np.uint8) & 0xF
        words = (c[..., 0::2] | (c[..., 1::2] << 4)).reshape(k // 512, 128, 2 * n)
    return np.ascontiguousarray(words), np.ascontiguousarray(byte.astype(np.uint8).reshape(k // 512, 16, n))


def unpack_weight(words, scales, fmt):
    g, _, n = scales.shape
    words = np.ascontiguousarray(words).reshape(g, 128, n, -1)
    if fmt == "e4m3":
        vals = words.view(ml_dtypes.float8_e4m3fn).astype(np.float64)
    else:
        nib = np.empty((g, 128, n, 4), np.uint8)
        nib[..., 0::2] = words & 0xF
        nib[..., 1::2] = words >> 4
        vals = E2M1[nib]
    vals = vals * np.repeat(np.exp2(scales.astype(np.float64) - 127.0), 8, axis=1)[..., None]
    return vals.transpose(0, 1, 3, 2).reshape(g * 512, n)


def gelu(v):
    return 0.5 * v * (1.0 + np.tanh(np.sqrt(2.0 / np.pi) * (v + 0.044715 * v**3)))


def bf(x):
    return np.asarray(x, np.float32).astype(ml_dtypes.bfloat16)


def planes(Y):
    n, m = Y.shape
    b = f64(bf(Y)).reshape(n // 32, 32, m)
    amax = np.abs(b).max(1)
    byte = np.clip(np.where(amax > 0, np.frexp(amax)[1] - 1 + 127 - 7, 1), 1, 254)
    codes = (b * np.exp2(127.0 - byte)[:, None, :]).reshape(n, m).astype(np.float32).astype(ml_dtypes.float8_e4m3fn).view(np.uint8)
    words = codes.reshape(n // 512, 128, 4, m).transpose(0, 1, 3, 2)
    return np.ascontiguousarray(words), np.ascontiguousarray(byte.astype(np.uint8).reshape(n // 512, 16, m))


K, T, S, P, H, N = 1024, 2048, 1024, 512, 1024, 1024


def setup_inputs():
    n = np.random.standard_normal
    s = mx_kscale(K)[:, None]
    u = mx_kscale(H)[:, None]
    tab_words, tab_scales = pack_weight(n((K, T)) * s, "e4m3")
    w2_words, w2_scales = pack_weight(n((K, H)) / np.sqrt(K) / s * u.T, "e2m1")
    w3_words, w3_scales = pack_weight(n((H, N)) * np.exp(0.8 * n(N)) / np.sqrt(H) / u, "e4m3")
    return {
        "tab_words": tab_words, "tab_scales": tab_scales,
        "offs": striped(np.random.permutation(T)[:S]),
        "pos1": striped(np.random.permutation(S)[:P]),
        "pos2": striped(np.random.permutation(S)[:P]),
        "w1": (0.7 * n((K, H)) / np.sqrt(K) / s).astype(np.float32),
        "shift": np.random.uniform(-2.8, 1.6, H).astype(np.float32),
        "w2_words": w2_words, "w2_scales": w2_scales,
        "temp": np.random.uniform(0.4, 1.6, H).astype(np.float32),
        "anchor": (0.5 * n((H, P)) * u).astype(np.float32),
        "w3_words": w3_words, "w3_scales": w3_scales,
    }


def reference(tab_words, tab_scales, offs, pos1, pos2, w1, shift, w2_words, w2_scales,
              temp, anchor, w3_words, w3_scales):
    v = unpack_weight(tab_words, tab_scales, "e4m3")[:, unstriped(offs)]
    h = np.tanh((mxq(f64(w1), 0, "e4m3").T @ v) + f64(shift)[:, None])
    g = unpack_weight(w2_words, w2_scales, "e2m1").T @ v
    top = h.max(axis=1)
    a = np.exp(f64(temp)[:, None] * (h[:, unstriped(pos1)] - top[:, None]))
    c = g[:, unstriped(pos2)]
    f = a * c + f64(anchor)
    y = unpack_weight(w3_words, w3_scales, "e4m3").T @ mxq(f, 0, "e4m3")
    words, scales = planes(y)
    return y, words, scales

@@ -1,0 +1,287 @@
+from contextlib import ExitStack
+
+import concourse.mybir as mybir
+
+K, T, S, PAIRS, H, N = 1024, 2048, 1024, 512, 1024, 1024
+FLOPS = 2 * K * H * S * 2 + 2 * H * N * PAIRS
+
+F32 = mybir.dt.float32
+BF16 = mybir.dt.bfloat16
+I32 = mybir.dt.int32
+U32 = mybir.dt.uint32
+U16 = mybir.dt.uint16
+U8 = mybir.dt.uint8
+FP8X4 = mybir.dt.float8_e4m3fn_x4
+FP4X4 = mybir.dt.float4_e2m1fn_x4
+ACT = mybir.ActivationFunctionType
+ALU = mybir.AluOpType
+AXIS = mybir.AxisListType
+
+P = 128
+PACK = 4
+PASS = P * PACK
+BANK = 512
+HALF = PAIRS // 2
+
+
+def tile_list_peptide_run_features_kernel(
+    tc, tab_words, tab_scales, offs, pos1, pos2, w1, shift, w2_words, w2_scales,
+    temp, anchor, w3_words, w3_scales, out_0, out_1, out_2,
+):
+    nc = tc.nc
+    with ExitStack() as ctx:
+        lists = ctx.enter_context(tc.tile_pool(name="lists", bufs=1))
+        keep = ctx.enter_context(tc.tile_pool(name="keep", bufs=1))
+        ring = ctx.enter_context(tc.tile_pool(name="ring", bufs=2))
+        psum = ctx.enter_context(tc.psum_pool(name="psum", bufs=8))
+
+        def held(shape, dtype, name):
+            return keep.tile(shape, dtype, name=name, align_bytes=64)
+
+        offs_sb = lists.tile([P, S // 16], U16, name="offs_sb")
+        pos1_sb = lists.tile([P, PAIRS // 16], U16, name="pos1_sb")
+        pos2_sb = lists.tile([P, PAIRS // 16], U16, name="pos2_sb")
+
+        tab_w = [held([P, T], U32, "tab_w%d" % a) for a in range(2)]
+        tab_s = held([P, 2 * T], U8, "tab_s")
+        v_w = [held([P, S], U32, "v_w%d" % a) for a in range(2)]
+        v_s = [held([P, S], U8, "v_s%d" % a) for a in range(2)]
+        w2_raw = held([P, 2 * 2 * H], U8, "w2_raw")
+        w2_w = [held([P, 2 * 2 * PASS], U8, "w2_w%d" % b) for b in range(2)]
+        w2s_raw = held([P, 2 * H], U8, "w2s_raw")
+        w2_s = held([P, 2 * H], U8, "w2_s")
+        w1_raw = {(a, b): ring.tile([P, PACK, PASS], F32, name="w1_raw", tag="staged", bufs=4) for b in range(2) for a in range(2)}
+        w1_w = [[held([P, PASS], U32, "w1_w%d%d" % (a, b)) for b in range(2)] for a in range(2)]
+        w1_s = [[held([P, PASS], U8, "w1_s%d%d" % (a, b)) for b in range(2)] for a in range(2)]
+        w3_raw = held([P, 2 * N], U32, "w3_raw")
+        w3_w = [held([P, N], U32, "w3_w%d" % b) for b in range(2)]
+        w3s_raw = held([P, N], U8, "w3s_raw")
+        w3_s = held([P, N], U8, "w3_s")
+        shift_sb = held([P, 2, PACK], F32, "shift_sb")
+        temp_sb = held([P, 2, PACK], F32, "temp_sb")
+        top = held([P, 2, PACK], F32, "top")
+        bias = held([P, 2, PACK], F32, "bias")
+        anchor_sb = [held([P, PACK, PAIRS], F32, "anchor%d" % b) for b in range(2)]
+        h_sb = {}
+        g_sb = [held([P, S], F32, "g%d" % i) for i in range(8)]
+        f_w = [held([P, PAIRS], U32, "f_w%d" % b) for b in range(2)]
+        f_s = [held([P, PAIRS], U8, "f_s%d" % b) for b in range(2)]
+        y_w = [held([P, PAIRS], U32, "y_w%d" % g) for g in range(2)]
+        y_s = held([P, 2, PAIRS], U8, "y_s")
+
+        nc.vector.memset(tab_s[:, 0:5 * T // 4].bitcast(I32), 0)
+        nc.gpsimd.memset(tab_s[:, 5 * T // 4:2 * T].bitcast(I32), 0)
+        nc.vector.memset(w2s_raw[:].bitcast(I32), 0)
+        nc.gpsimd.memset(w3s_raw[:].bitcast(I32), 0)
+        nc.sync.dma_start(offs_sb[:], offs)
+        nc.sync.dma_start(pos1_sb[:], pos1)
+        nc.sync.dma_start(pos2_sb[:], pos2)
+        nc.sync.dma_start(shift_sb[:], shift.rearrange("(b p t) -> p b t", b=2, t=PACK))
+        nc.sync.dma_start(temp_sb[:], temp.rearrange("(b p t) -> p b t", b=2, t=PACK))
+
+        def load_table(a):
+            nc.sync.dma_start(tab_w[a][:].bitcast(I32), tab_words[a].rearrange("p n t -> p (n t)").bitcast(I32))
+
+        def load_w1(a, b):
+            rows = w1[PASS * a:PASS * (a + 1), PASS * b:PASS * (b + 1)]
+            nc.sync.dma_start(w1_raw[a, b][:], rows.rearrange("(p j) c -> p j c", j=PACK))
+
+        def load_anchor(b):
+            nc.sync.dma_start(anchor_sb[b][:], anchor[PASS * b:PASS * (b + 1), :].rearrange("(p t) m -> p t m", t=PACK))
+
+        load_table(0)
+        nc.sync.dma_start(w2_raw[:].bitcast(I32).rearrange("p (a c) -> p a c", a=2),
+                          w2_words.bitcast(I32).rearrange("a p c -> p a c"))
+        for q in range(4):
+            nc.sync.dma_start(
+                tab_s[32 * q:32 * q + 4, :].bitcast(I32).rearrange("r (a c) -> r a c", a=2),
+                tab_scales[:, 4 * q:4 * q + 4, :].bitcast(I32).rearrange("a r c -> r a c"))
+        for q in range(4):
+            nc.sync.dma_start(
+                w2s_raw[32 * q:32 * q + 4, :].bitcast(I32).rearrange("r (a c) -> r a c", a=2),
+                w2_scales[:, 4 * q:4 * q + 4, :].bitcast(I32).rearrange("a r c -> r a c"))
+        load_w1(0, 0)
+        load_w1(1, 0)
+        load_table(1)
+        load_w1(0, 1)
+        load_w1(1, 1)
+        load_anchor(0)
+        nc.sync.dma_start(w3_raw[:].bitcast(I32).rearrange("p (b c) -> p b c", b=2),
+                          w3_words.rearrange("b p n t -> p b (n t)").bitcast(I32))
+        for q in range(4):
+            nc.sync.dma_start(w3s_raw[32 * q:32 * q + 8, :].bitcast(I32), w3_scales[:, 4 * q:4 * q + 4, :].bitcast(I32))
+        load_anchor(1)
+
+        def gather_words(a, j0, j1):
+            nc.vector.tensor_copy(v_w[a][:, j0:j1], tab_w[a][:].indirect(offs_sb[:, j0 // 16:j1 // 16]))
+
+        def gather_scales(a):
+            nc.vector.tensor_copy(v_s[a][:], tab_s[:, T * a:T * (a + 1)].indirect(offs_sb[:]))
+
+        def deal_w2(b):
+            src = w2_raw[:].bitcast(U16).rearrange("p (a b m t) -> p b a m t", a=2, b=2, t=PACK)[:, b]
+            dst = w2_w[b][:].bitcast(U16).rearrange("p (a t m) -> p a m t", a=2, t=PACK)
+            nc.scalar.copy(dst, src)
+
+        def deal_w3(b):
+            src = w3_raw[:, N * b:N * (b + 1)].rearrange("p (g m t) -> p g m t", g=2, t=PACK)
+            dst = w3_w[b][:].rearrange("p (g t m) -> p g m t", g=2, t=PACK)
+            nc.scalar.copy(dst, src)
+
+        def deal_scales(dst, src):
+            nc.vector.tensor_copy(dst[:].rearrange("p (x t m) -> p x m t", t=PACK, m=P),
+                                  src[:].rearrange("p (x m t) -> p x m t", t=PACK, m=P))
+
+        w1_bf = {}
+
+        def round_w1(a, b, copy):
+            w1_bf[a, b] = ring.tile([P, PACK * PASS], BF16, name="w1_bf", align_bytes=64)
+            copy(w1_bf[a, b][:].rearrange("p (t m j) -> p m j t", t=PACK, j=PACK),
+                 w1_raw[a, b][:].rearrange("p j (m t) -> p m j t", t=PACK))
+
+        def quantise_w1(a, b):
+            nc.vector.quantize_mx(out=w1_w[a][b][:].bitcast(FP8X4), scales=w1_s[a][b][:], in_=w1_bf[a, b][:])
+
+        def g_step(i, c):
+            b, t = divmod(i, PACK)
+            cols = slice(BANK * c, BANK * (c + 1))
+            acc = psum.tile([P, BANK], F32, name="acc")
+            for a in range(2):
+                first = PASS * a + P * t
+                nc.tensor.matmul_mx(
+                    out=acc[:],
+                    lhsT=w2_w[b][:, 2 * first:2 * (first + P)].bitcast(FP4X4),
+                    lhsT_scale=w2_s[:, H * a + PASS * b + P * t:H * a + PASS * b + P * (t + 1)],
+                    rhs=v_w[a][:, cols].bitcast(FP8X4),
+                    rhs_scale=v_s[a][:, cols],
+                    start=(a == 0), stop=(a == 1))
+            nc.scalar.copy(g_sb[i][:, cols], acc[:])
+
+        def h_step(i):
+            b, t = divmod(i, PACK)
+            h_sb[i] = ring.tile([P, S], F32, name="h_sb", bufs=6)
+            for c in range(2):
+                cols = slice(BANK * c, BANK * (c + 1))
+                acc = psum.tile([P, BANK], F32, name="acc")
+                for a in range(2):
+                    nc.tensor.matmul_mx(
+                        out=acc[:],
+                        lhsT=w1_w[a][b][:, P * t:P * (t + 1)].bitcast(FP8X4),
+                        lhsT_scale=w1_s[a][b][:, P * t:P * (t + 1)],
+                        rhs=v_w[a][:, cols].bitcast(FP8X4),
+                        rhs_scale=v_s[a][:, cols],
+                        start=(a == 0), stop=(a == 1))
+                nc.scalar.activation(h_sb[i][:, cols], acc[:], ACT.Tanh, bias=shift_sb[:, b, t:t + 1])
+            nc.vector.reduce_max(top[:, b, t:t + 1], h_sb[i][:], axis=AXIS.X)
+            nc.gpsimd.tensor_scalar(bias[:, b, t:t + 1], top[:, b, t:t + 1], temp_sb[:, b, t:t + 1], -1.0,
+                                    op0=ALU.mult, op1=ALU.mult)
+
+        prod = {}
+
+        def pair_step(i, m0, m1):
+            b, t = divmod(i, PACK)
+            if t == 0:
+                prod[b, m0] = ring.tile([P, PACK, m1 - m0], F32, name="prod")
+            entries = slice(m0 // 16, m1 // 16)
+            look = ring.tile([P, m1 - m0], F32, name="look", bufs=3)
+            nc.scalar.activation(look[:], h_sb[i][:].indirect(pos1_sb[:, entries]), ACT.Exp,
+                                 bias=bias[:, b, t:t + 1], scale=temp_sb[:, b, t:t + 1])
+            nc.vector.tensor_tensor(prod[b, m0][:, t, :], g_sb[i][:].indirect(pos2_sb[:, entries]), look[:], ALU.mult)
+
+        f_bf = {}
+
+        def join(b, m0, m1):
+            f_bf[b, m0] = ring.tile([P, PACK * (m1 - m0)], BF16, name="f_bf", align_bytes=64)
+            nc.vector.tensor_tensor(
+                f_bf[b, m0][:].rearrange("p (c i t) -> p c t i", i=4, t=PACK),
+                prod[b, m0][:].rearrange("p t (c i) -> p c t i", i=4),
+                anchor_sb[b][:, :, m0:m1].rearrange("p t (c i) -> p c t i", i=4), ALU.add)
+
+        def quantise_f(b, m0, m1):
+            nc.vector.quantize_mx(out=f_w[b][:, m0:m1].bitcast(FP8X4), scales=f_s[b][:, m0:m1], in_=f_bf[b, m0][:])
+
+        y_sb = {}
+        y_bf = {}
+
+        def y_step(g, m0):
+            cols = slice(m0, m0 + HALF)
+            y_sb[g, m0] = ring.tile([P, PACK, HALF], F32, name="y_sb", tag="staged", bufs=4)
+            for u in range(2):
+                acc = psum.tile([P, 2, HALF], F32, name="acc")
+                for e in range(2):
+                    first = PASS * g + P * (2 * u + e)
+                    for b in range(2):
+                        nc.tensor.matmul_mx(
+                            out=acc[:, e, :],
+                            lhsT=w3_w[b][:, first:first + P].bitcast(FP8X4),
+                            lhsT_scale=w3_s[4 * b:, first:first + P],
+                            rhs=f_w[b][:, cols].bitcast(FP8X4),
+                            rhs_scale=f_s[b][:, cols],
+                            start=(b == 0), stop=(b == 1))
+                nc.scalar.copy(y_sb[g, m0][:, 2 * u:2 * u + 2, :], acc[:])
+            nc.sync.dma_start(out_0[PASS * g:PASS * (g + 1), cols].rearrange("(p t) m -> p t m", t=PACK), y_sb[g, m0][:])
+
+        def round_y(g, m0):
+            y_bf[g, m0] = ring.tile([P, PACK * HALF], BF16, name="y_bf", align_bytes=64)
+            nc.vector.tensor_copy(y_bf[g, m0][:].rearrange("p (c i t) -> p c t i", i=4, t=PACK),
+                                  y_sb[g, m0][:].rearrange("p t (c i) -> p c t i", i=4))
+
+        def quantise_y(g, m0):
+            cols = slice(m0, m0 + HALF)
+            nc.vector.quantize_mx(out=y_w[g][:, cols].bitcast(FP8X4), scales=y_s[:, g, cols], in_=y_bf[g, m0][:])
+            nc.sync.dma_start(out_1[g].rearrange("p m t -> p (m t)").bitcast(I32)[:, cols], y_w[g][:, cols].bitcast(I32))
+
+        gather_words(0, 0, S)
+        gather_scales(0)
+        gather_scales(1)
+        deal_scales(w2_s, w2s_raw)
+        deal_w2(0)
+        deal_w2(1)
+        round_w1(0, 0, nc.scalar.copy)
+        round_w1(1, 0, nc.scalar.copy)
+        quantise_w1(0, 0)
+        gather_words(1, 0, BANK)
+        quantise_w1(1, 0)
+        gather_words(1, BANK, S)
+        for i in range(8):
+            h_step(i)
+            g_step(i, 0)
+            g_step(i, 1)
+            if i >= 1:
+                pair_step(i - 1, 0, PAIRS if i <= PACK else HALF)
+            if i < 2:
+                round_w1(i, 1, nc.vector.tensor_copy)
+            if 1 <= i < 3:
+                quantise_w1(i - 1, 1)
+            if i == 3:
+                deal_scales(w3_s, w3s_raw)
+            if i == 5:
+                join(0, 0, PAIRS)
+                deal_w3(0)
+            if i == 6:
+                quantise_f(0, 0, PAIRS)
+                deal_w3(1)
+        pair_step(7, 0, HALF)
+        pair_step(4, HALF, PAIRS)
+        join(1, 0, HALF)
+        pair_step(5, HALF, PAIRS)
+        quantise_f(1, 0, HALF)
+        pair_step(6, HALF, PAIRS)
+        pair_step(7, HALF, PAIRS)
+        y_step(0, 0)
+        y_step(1, 0)
+        join(1, HALF, PAIRS)
+        round_y(0, 0)
+        quantise_f(1, HALF, PAIRS)
+        y_step(0, HALF)
+        round_y(1, 0)
+        quantise_y(0, 0)
+        y_step(1, HALF)
+        quantise_y(1, 0)
+        round_y(0, HALF)
+        quantise_y(0, HALF)
+        round_y(1, HALF)
+        quantise_y(1, HALF)
+        for q in range(4):
+            nc.scalar.dma_start(out_2[:, 4 * q:4 * q + 4, :].bitcast(I32).rearrange("g r m -> r g m"),
+                                y_s[32 * q:32 * q + 4, :, :].bitcast(I32))

@@ -22,6 +22,13 @@ PACK = 4
 PASS = P * PACK
 BANK = 512
 HALF = PAIRS // 2
+ROW_TILES = H // P
+QUADRANTS = 4
+RUN = 4
+
+G_AHEAD = 5
+LAG = 2
+PASS0_FIRST = 2
 
 
 def tile_list_peptide_run_features_kernel(
@@ -38,106 +45,79 @@ def tile_list_peptide_run_features_kernel(
         def held(shape, dtype, name):
             return keep.tile(shape, dtype, name=name, align_bytes=64)
 
+        def shared(shape, dtype, name, place):
+            return keep.tile(shape, dtype, name=name, tag=place, align_bytes=64)
+
         offs_sb = lists.tile([P, S // 16], U16, name="offs_sb")
         pos1_sb = lists.tile([P, PAIRS // 16], U16, name="pos1_sb")
         pos2_sb = lists.tile([P, PAIRS // 16], U16, name="pos2_sb")
 
-        tab_w = [held([P, T], U32, "tab_w%d" % a) for a in range(2)]
-        tab_s = held([P, 2 * T], U8, "tab_s")
+        tab_w = [shared([P, T], U32, "tab_w%d" % a, "place_tab%d" % a) for a in range(2)]
+        tab_s = shared([P, T], U8, "tab_s", "place_tab_s")
         v_w = [held([P, S], U32, "v_w%d" % a) for a in range(2)]
         v_s = [held([P, S], U8, "v_s%d" % a) for a in range(2)]
-        w2_raw = held([P, 2 * 2 * H], U8, "w2_raw")
+        w2_raw = shared([P, 2 * 2 * H], U8, "w2_raw", "place_w2")
         w2_w = [held([P, 2 * 2 * PASS], U8, "w2_w%d" % b) for b in range(2)]
-        w2s_raw = held([P, 2 * H], U8, "w2s_raw")
+        raw_s = held([P, 2 * H], U8, "raw_s")
         w2_s = held([P, 2 * H], U8, "w2_s")
-        w1_raw = {(a, b): ring.tile([P, PACK, PASS], F32, name="w1_raw", tag="staged", bufs=4) for b in range(2) for a in range(2)}
         w1_w = [[held([P, PASS], U32, "w1_w%d%d" % (a, b)) for b in range(2)] for a in range(2)]
         w1_s = [[held([P, PASS], U8, "w1_s%d%d" % (a, b)) for b in range(2)] for a in range(2)]
-        w3_raw = held([P, 2 * N], U32, "w3_raw")
         w3_w = [held([P, N], U32, "w3_w%d" % b) for b in range(2)]
-        w3s_raw = held([P, N], U8, "w3s_raw")
         w3_s = held([P, N], U8, "w3_s")
-        shift_sb = held([P, 2, PACK], F32, "shift_sb")
-        temp_sb = held([P, 2, PACK], F32, "temp_sb")
-        top = held([P, 2, PACK], F32, "top")
-        bias = held([P, 2, PACK], F32, "bias")
-        anchor_sb = [held([P, PACK, PAIRS], F32, "anchor%d" % b) for b in range(2)]
-        h_sb = {}
-        g_sb = [held([P, S], F32, "g%d" % i) for i in range(8)]
+        look_bias = held([P, 2, PACK], F32, "look_bias")
+        g_sb = [held([P, S], F32, "g%d" % i) for i in range(ROW_TILES)]
         f_w = [held([P, PAIRS], U32, "f_w%d" % b) for b in range(2)]
         f_s = [held([P, PAIRS], U8, "f_s%d" % b) for b in range(2)]
         y_w = [held([P, PAIRS], U32, "y_w%d" % g) for g in range(2)]
         y_s = held([P, 2, PAIRS], U8, "y_s")
+        w1_raw, w1_bf, h_sb, prod, f_bf, y_sb, y_bf = {}, {}, {}, {}, {}, {}, {}
 
-        nc.vector.memset(tab_s[:, 0:5 * T // 4].bitcast(I32), 0)
-        nc.gpsimd.memset(tab_s[:, 5 * T // 4:2 * T].bitcast(I32), 0)
-        nc.vector.memset(w2s_raw[:].bitcast(I32), 0)
-        nc.gpsimd.memset(w3s_raw[:].bitcast(I32), 0)
+        nc.gpsimd.memset(tab_s[:].bitcast(I32), 0)
+        nc.vector.memset(raw_s[:].bitcast(I32), 0)
+        nc.gpsimd.memset(v_s[1][:].bitcast(I32), 0)
         nc.sync.dma_start(offs_sb[:], offs)
         nc.sync.dma_start(pos1_sb[:], pos1)
         nc.sync.dma_start(pos2_sb[:], pos2)
-        nc.sync.dma_start(shift_sb[:], shift.rearrange("(b p t) -> p b t", b=2, t=PACK))
-        nc.sync.dma_start(temp_sb[:], temp.rearrange("(b p t) -> p b t", b=2, t=PACK))
+        for q in range(QUADRANTS):
+            nc.sync.dma_start(tab_s[32 * q:32 * q + 8, :].bitcast(I32), tab_scales[:, 4 * q:4 * q + 4, :].bitcast(I32))
 
         def load_table(a):
             nc.sync.dma_start(tab_w[a][:].bitcast(I32), tab_words[a].rearrange("p n t -> p (n t)").bitcast(I32))
 
-        def load_w1(a, b):
-            rows = w1[PASS * a:PASS * (a + 1), PASS * b:PASS * (b + 1)]
-            nc.sync.dma_start(w1_raw[a, b][:], rows.rearrange("(p j) c -> p j c", j=PACK))
-
-        def load_anchor(b):
-            nc.sync.dma_start(anchor_sb[b][:], anchor[PASS * b:PASS * (b + 1), :].rearrange("(p t) m -> p t m", t=PACK))
+        def load_w1(a, b, place):
+            w1_raw[a, b] = shared([P, PACK, PASS], F32, "w1_raw%d%d" % (a, b), place)
+            part = w1[PASS * a:PASS * (a + 1), PASS * b:PASS * (b + 1)]
+            nc.sync.dma_start(w1_raw[a, b][:], part.rearrange("(p j) c -> p j c", j=PACK))
 
         load_table(0)
         nc.sync.dma_start(w2_raw[:].bitcast(I32).rearrange("p (a c) -> p a c", a=2),
                           w2_words.bitcast(I32).rearrange("a p c -> p a c"))
-        for q in range(4):
+        for q in range(QUADRANTS):
             nc.sync.dma_start(
-                tab_s[32 * q:32 * q + 4, :].bitcast(I32).rearrange("r (a c) -> r a c", a=2),
-                tab_scales[:, 4 * q:4 * q + 4, :].bitcast(I32).rearrange("a r c -> r a c"))
-        for q in range(4):
-            nc.sync.dma_start(
-                w2s_raw[32 * q:32 * q + 4, :].bitcast(I32).rearrange("r (a c) -> r a c", a=2),
+                raw_s[32 * q:32 * q + 4, :].bitcast(I32).rearrange("r (a c) -> r a c", a=2),
                 w2_scales[:, 4 * q:4 * q + 4, :].bitcast(I32).rearrange("a r c -> r a c"))
-        load_w1(0, 0)
-        load_w1(1, 0)
         load_table(1)
-        load_w1(0, 1)
-        load_w1(1, 1)
-        load_anchor(0)
-        nc.sync.dma_start(w3_raw[:].bitcast(I32).rearrange("p (b c) -> p b c", b=2),
-                          w3_words.rearrange("b p n t -> p b (n t)").bitcast(I32))
-        for q in range(4):
-            nc.sync.dma_start(w3s_raw[32 * q:32 * q + 8, :].bitcast(I32), w3_scales[:, 4 * q:4 * q + 4, :].bitcast(I32))
-        load_anchor(1)
+        row_values = held([P, 2, 2, PACK], F32, "row_values")
+        for which, values in enumerate((shift, temp)):
+            nc.sync.dma_start(row_values[:, which], values.rearrange("(b p t) -> p b t", b=2, t=PACK))
+        shift_sb, temp_sb = row_values[:, 0], row_values[:, 1]
 
         def gather_words(a, j0, j1):
             nc.vector.tensor_copy(v_w[a][:, j0:j1], tab_w[a][:].indirect(offs_sb[:, j0 // 16:j1 // 16]))
 
-        def gather_scales(a):
-            nc.vector.tensor_copy(v_s[a][:], tab_s[:, T * a:T * (a + 1)].indirect(offs_sb[:]))
+        def deal_scales(dst, src):
+            nc.vector.tensor_copy(dst.rearrange("p (x t m) -> p x t m", t=PACK, m=P),
+                                  src.rearrange("p (x m t) -> p x t m", t=PACK, m=P))
 
         def deal_w2(b):
-            src = w2_raw[:].bitcast(U16).rearrange("p (a b m t) -> p b a m t", a=2, b=2, t=PACK)[:, b]
-            dst = w2_w[b][:].bitcast(U16).rearrange("p (a t m) -> p a m t", a=2, t=PACK)
+            src = w2_raw[:].bitcast(U16).rearrange("p (a b m t) -> p b a t m", a=2, b=2, t=PACK)[:, b]
+            dst = w2_w[b][:].bitcast(U16).rearrange("p (a t m) -> p a t m", a=2, t=PACK)
             nc.scalar.copy(dst, src)
 
-        def deal_w3(b):
-            src = w3_raw[:, N * b:N * (b + 1)].rearrange("p (g m t) -> p g m t", g=2, t=PACK)
-            dst = w3_w[b][:].rearrange("p (g t m) -> p g m t", g=2, t=PACK)
-            nc.scalar.copy(dst, src)
-
-        def deal_scales(dst, src):
-            nc.vector.tensor_copy(dst[:].rearrange("p (x t m) -> p x m t", t=PACK, m=P),
-                                  src[:].rearrange("p (x m t) -> p x m t", t=PACK, m=P))
-
-        w1_bf = {}
-
-        def round_w1(a, b, copy):
+        def round_w1(a, b):
             w1_bf[a, b] = ring.tile([P, PACK * PASS], BF16, name="w1_bf", align_bytes=64)
-            copy(w1_bf[a, b][:].rearrange("p (t m j) -> p m j t", t=PACK, j=PACK),
-                 w1_raw[a, b][:].rearrange("p j (m t) -> p m j t", t=PACK))
+            nc.vector.tensor_copy(w1_bf[a, b][:].rearrange("p (u e m j) -> p u m j e", u=2, e=2, j=PACK),
+                                  w1_raw[a, b][:].rearrange("p j (m u e) -> p u m j e", u=2, e=2))
 
         def quantise_w1(a, b):
             nc.vector.quantize_mx(out=w1_w[a][b][:].bitcast(FP8X4), scales=w1_s[a][b][:], in_=w1_bf[a, b][:])
@@ -146,18 +126,20 @@ def tile_list_peptide_run_features_kernel(
             b, t = divmod(i, PACK)
             cols = slice(BANK * c, BANK * (c + 1))
             acc = psum.tile([P, BANK], F32, name="acc")
-            for a in range(2):
-                first = PASS * a + P * t
+            passes = (0, 1) if (c == 0 and i < PASS0_FIRST) else (1, 0)
+            for a in passes:
+                word0 = PASS * a + P * t
+                scale0 = H * a + PASS * b + P * t
                 nc.tensor.matmul_mx(
                     out=acc[:],
-                    lhsT=w2_w[b][:, 2 * first:2 * (first + P)].bitcast(FP4X4),
-                    lhsT_scale=w2_s[:, H * a + PASS * b + P * t:H * a + PASS * b + P * (t + 1)],
+                    lhsT=w2_w[b][:, 2 * word0:2 * (word0 + P)].bitcast(FP4X4),
+                    lhsT_scale=w2_s[:, scale0:scale0 + P],
                     rhs=v_w[a][:, cols].bitcast(FP8X4),
                     rhs_scale=v_s[a][:, cols],
-                    start=(a == 0), stop=(a == 1))
+                    start=(a == passes[0]), stop=(a == passes[1]))
             nc.scalar.copy(g_sb[i][:, cols], acc[:])
 
-        def h_step(i):
+        def h_step(i, top):
             b, t = divmod(i, PACK)
             h_sb[i] = ring.tile([P, S], F32, name="h_sb", bufs=6)
             for c in range(2):
@@ -169,119 +151,125 @@ def tile_list_peptide_run_features_kernel(
                         lhsT=w1_w[a][b][:, P * t:P * (t + 1)].bitcast(FP8X4),
                         lhsT_scale=w1_s[a][b][:, P * t:P * (t + 1)],
                         rhs=v_w[a][:, cols].bitcast(FP8X4),
-                        rhs_scale=v_s[a][:, cols],
+                        rhs_scale=v_s[0][4 * a:, cols],
                         start=(a == 0), stop=(a == 1))
                 nc.scalar.activation(h_sb[i][:, cols], acc[:], ACT.Tanh, bias=shift_sb[:, b, t:t + 1])
             nc.vector.reduce_max(top[:, b, t:t + 1], h_sb[i][:], axis=AXIS.X)
-            nc.gpsimd.tensor_scalar(bias[:, b, t:t + 1], top[:, b, t:t + 1], temp_sb[:, b, t:t + 1], -1.0,
+            nc.vector.tensor_scalar(look_bias[:, b, t:t + 1], top[:, b, t:t + 1], temp_sb[:, b, t:t + 1], -1.0,
                                     op0=ALU.mult, op1=ALU.mult)
-
-        prod = {}
 
         def pair_step(i, m0, m1):
             b, t = divmod(i, PACK)
-            if t == 0:
-                prod[b, m0] = ring.tile([P, PACK, m1 - m0], F32, name="prod")
+            if b not in prod:
+                prod[b] = ring.tile([P, PACK, PAIRS], F32, name="prod")
             entries = slice(m0 // 16, m1 // 16)
             look = ring.tile([P, m1 - m0], F32, name="look", bufs=3)
             nc.scalar.activation(look[:], h_sb[i][:].indirect(pos1_sb[:, entries]), ACT.Exp,
-                                 bias=bias[:, b, t:t + 1], scale=temp_sb[:, b, t:t + 1])
-            nc.vector.tensor_tensor(prod[b, m0][:, t, :], g_sb[i][:].indirect(pos2_sb[:, entries]), look[:], ALU.mult)
+                                 bias=look_bias[:, b, t:t + 1], scale=temp_sb[:, b, t:t + 1])
+            nc.vector.tensor_tensor(prod[b][:, t, m0:m1], g_sb[i][:].indirect(pos2_sb[:, entries]), look[:], ALU.mult)
 
-        f_bf = {}
-
-        def join(b, m0, m1):
-            f_bf[b, m0] = ring.tile([P, PACK * (m1 - m0)], BF16, name="f_bf", align_bytes=64)
+        def make_f(b, m0, anchor_sb):
+            cols = slice(m0, m0 + HALF)
+            f_bf[b, m0] = ring.tile([P, PACK * HALF], BF16, name="f_bf", align_bytes=64)
             nc.vector.tensor_tensor(
-                f_bf[b, m0][:].rearrange("p (c i t) -> p c t i", i=4, t=PACK),
-                prod[b, m0][:].rearrange("p t (c i) -> p c t i", i=4),
-                anchor_sb[b][:, :, m0:m1].rearrange("p t (c i) -> p c t i", i=4), ALU.add)
-
-        def quantise_f(b, m0, m1):
-            nc.vector.quantize_mx(out=f_w[b][:, m0:m1].bitcast(FP8X4), scales=f_s[b][:, m0:m1], in_=f_bf[b, m0][:])
-
-        y_sb = {}
-        y_bf = {}
+                f_bf[b, m0][:].rearrange("p (c i t) -> p c t i", i=RUN, t=PACK),
+                prod[b][:, :, cols].rearrange("p t (c i) -> p c t i", i=RUN),
+                anchor_sb[:, b].rearrange("p (t c i) -> p c t i", t=PACK, i=RUN)[:, m0 // RUN:(m0 + HALF) // RUN],
+                ALU.add)
+            nc.vector.quantize_mx(out=f_w[b][:, cols].bitcast(FP8X4), scales=f_s[b][:, cols], in_=f_bf[b, m0][:])
 
         def y_step(g, m0):
             cols = slice(m0, m0 + HALF)
-            y_sb[g, m0] = ring.tile([P, PACK, HALF], F32, name="y_sb", tag="staged", bufs=4)
-            for u in range(2):
+            y_sb[g, m0] = ring.tile([P, PACK, HALF], F32, name="y_sb", bufs=4)
+            for t0 in range(0, PACK, 2):
                 acc = psum.tile([P, 2, HALF], F32, name="acc")
-                for e in range(2):
-                    first = PASS * g + P * (2 * u + e)
-                    for b in range(2):
+                for b in range(2):
+                    for e in range(2):
+                        word0 = PASS * g + P * (t0 + e)
                         nc.tensor.matmul_mx(
                             out=acc[:, e, :],
-                            lhsT=w3_w[b][:, first:first + P].bitcast(FP8X4),
-                            lhsT_scale=w3_s[4 * b:, first:first + P],
+                            lhsT=w3_w[b][:, word0:word0 + P].bitcast(FP8X4),
+                            lhsT_scale=w3_s[4 * b:, word0:word0 + P],
                             rhs=f_w[b][:, cols].bitcast(FP8X4),
                             rhs_scale=f_s[b][:, cols],
-                            start=(b == 0), stop=(b == 1))
-                nc.scalar.copy(y_sb[g, m0][:, 2 * u:2 * u + 2, :], acc[:])
+                            start=(b == 0 and e == 0), stop=(b == 1 and e == 1))
+                nc.scalar.copy(y_sb[g, m0][:, t0:t0 + 2, :], acc[:])
             nc.sync.dma_start(out_0[PASS * g:PASS * (g + 1), cols].rearrange("(p t) m -> p t m", t=PACK), y_sb[g, m0][:])
 
-        def round_y(g, m0):
-            y_bf[g, m0] = ring.tile([P, PACK * HALF], BF16, name="y_bf", align_bytes=64)
-            nc.vector.tensor_copy(y_bf[g, m0][:].rearrange("p (c i t) -> p c t i", i=4, t=PACK),
-                                  y_sb[g, m0][:].rearrange("p t (c i) -> p c t i", i=4))
-
-        def quantise_y(g, m0):
+        def make_planes(g, m0):
             cols = slice(m0, m0 + HALF)
+            y_bf[g, m0] = ring.tile([P, PACK * HALF], BF16, name="y_bf", align_bytes=64)
+            nc.vector.tensor_copy(y_bf[g, m0][:].rearrange("p (c i t) -> p c t i", i=RUN, t=PACK),
+                                  y_sb[g, m0][:].rearrange("p t (c i) -> p c t i", i=RUN))
             nc.vector.quantize_mx(out=y_w[g][:, cols].bitcast(FP8X4), scales=y_s[:, g, cols], in_=y_bf[g, m0][:])
-            nc.sync.dma_start(out_1[g].rearrange("p m t -> p (m t)").bitcast(I32)[:, cols], y_w[g][:, cols].bitcast(I32))
 
+        nc.vector.tensor_copy(v_s[0][:], tab_s[:].indirect(offs_sb[:]))
+        for q in range(QUADRANTS):
+            nc.sync.dma_start(v_s[1][32 * q:32 * q + 4, :].bitcast(I32), v_s[0][32 * q + 4:32 * q + 8, :].bitcast(I32))
+        load_w1(0, 0, "place_tab_s")
         gather_words(0, 0, S)
-        gather_scales(0)
-        gather_scales(1)
-        deal_scales(w2_s, w2s_raw)
+        load_w1(1, 0, "place_tab0")
+        deal_scales(w2_s[:], raw_s[:])
         deal_w2(0)
         deal_w2(1)
-        round_w1(0, 0, nc.scalar.copy)
-        round_w1(1, 0, nc.scalar.copy)
-        quantise_w1(0, 0)
+        load_w1(0, 1, "place_w2")
         gather_words(1, 0, BANK)
-        quantise_w1(1, 0)
         gather_words(1, BANK, S)
-        for i in range(8):
-            h_step(i)
-            g_step(i, 0)
-            g_step(i, 1)
-            if i >= 1:
-                pair_step(i - 1, 0, PAIRS if i <= PACK else HALF)
-            if i < 2:
-                round_w1(i, 1, nc.vector.tensor_copy)
-            if 1 <= i < 3:
-                quantise_w1(i - 1, 1)
-            if i == 3:
-                deal_scales(w3_s, w3s_raw)
-            if i == 5:
-                join(0, 0, PAIRS)
-                deal_w3(0)
-            if i == 6:
-                quantise_f(0, 0, PAIRS)
-                deal_w3(1)
-        pair_step(7, 0, HALF)
-        pair_step(4, HALF, PAIRS)
-        join(1, 0, HALF)
-        pair_step(5, HALF, PAIRS)
-        quantise_f(1, 0, HALF)
-        pair_step(6, HALF, PAIRS)
-        pair_step(7, HALF, PAIRS)
+        load_w1(1, 1, "place_tab1")
+        for q in range(QUADRANTS):
+            nc.sync.dma_start(raw_s[32 * q:32 * q + 8, 0:N].bitcast(I32), w3_scales[:, 4 * q:4 * q + 4, :].bitcast(I32))
+        for a in range(2):
+            round_w1(a, 0)
+            quantise_w1(a, 0)
+        w3_raw = shared([P, 2 * N], U32, "w3_raw", "place_tab0")
+        nc.sync.dma_start(w3_raw[:].bitcast(I32).rearrange("p (b c) -> p b c", b=2),
+                          w3_words.rearrange("b p n t -> p b (n t)").bitcast(I32))
+        round_w1(0, 1)
+        quantise_w1(0, 1)
+        anchor_sb = shared([P, 2, PACK * PAIRS], F32, "anchor_sb", "place_w2")
+        nc.sync.dma_start(anchor_sb[:], anchor.rearrange("(b p t) m -> p b (t m)", b=2, t=PACK))
+        round_w1(1, 1)
+        quantise_w1(1, 1)
+
+        for c in range(2):
+            for i in range(G_AHEAD):
+                g_step(i, c)
+        top = shared([P, 2, PACK], F32, "top", "place_tab1")
+        for i in range(ROW_TILES):
+            h_step(i, top)
+            behind = i - LAG
+            if behind >= G_AHEAD:
+                for c in range(2):
+                    g_step(behind, c)
+            if behind >= 0:
+                pair_step(behind, 0, PAIRS)
+            if i == PACK - 1:
+                deal_scales(w3_s[:], raw_s[:, 0:N])
+            if behind >= PACK:
+                make_f(0, HALF * (behind - PACK), anchor_sb)
+
+        last = range(ROW_TILES - LAG, ROW_TILES)
+        for i in last:
+            for c in range(2):
+                g_step(i, c)
+        for i in last:
+            pair_step(i, 0, HALF)
+        for b in range(2):
+            nc.scalar.copy(w3_w[b][:].rearrange("p (g t m) -> p g m t", g=2, t=PACK),
+                           w3_raw[:, N * b:N * (b + 1)].rearrange("p (g m t) -> p g m t", g=2, t=PACK))
+        make_f(1, 0, anchor_sb)
+        for i in last:
+            pair_step(i, HALF, PAIRS)
         y_step(0, 0)
-        y_step(1, 0)
-        join(1, HALF, PAIRS)
-        round_y(0, 0)
-        quantise_f(1, HALF, PAIRS)
-        y_step(0, HALF)
-        round_y(1, 0)
-        quantise_y(0, 0)
-        y_step(1, HALF)
-        quantise_y(1, 0)
-        round_y(0, HALF)
-        quantise_y(0, HALF)
-        round_y(1, HALF)
-        quantise_y(1, HALF)
-        for q in range(4):
+        make_f(1, HALF, anchor_sb)
+        pieces = [(g, m0) for m0 in (0, HALF) for g in range(2)]
+        for g, m0 in pieces[1:]:
+            y_step(g, m0)
+        for g, m0 in pieces:
+            make_planes(g, m0)
+
+        for g in range(2):
+            nc.sync.dma_start(out_1[g].rearrange("p m t -> p (m t)").bitcast(I32), y_w[g][:].bitcast(I32))
+        for q in range(QUADRANTS):
             nc.scalar.dma_start(out_2[:, 4 * q:4 * q + 4, :].bitcast(I32).rearrange("g r m -> r g m"),
                                 y_s[32 * q:32 * q + 4, :, :].bitcast(I32))

@@ -65,6 +65,7 @@ def tile_list_peptide_run_features_kernel(
         w3_w = [held([P, N], U32, "w3_w%d" % b) for b in range(2)]
         w3_s = held([P, N], U8, "w3_s")
         look_bias = held([P, 2, PACK], F32, "look_bias")
+        minus_temp = held([P, 2, PACK], F32, "minus_temp")
         g_sb = [held([P, S], F32, "g%d" % i) for i in range(ROW_TILES)]
         f_w = [held([P, PAIRS], U32, "f_w%d" % b) for b in range(2)]
         f_s = [held([P, PAIRS], U8, "f_s%d" % b) for b in range(2)]
@@ -155,8 +156,7 @@ def tile_list_peptide_run_features_kernel(
                         start=(a == 0), stop=(a == 1))
                 nc.scalar.activation(h_sb[i][:, cols], acc[:], ACT.Tanh, bias=shift_sb[:, b, t:t + 1])
             nc.vector.reduce_max(top[:, b, t:t + 1], h_sb[i][:], axis=AXIS.X)
-            nc.vector.tensor_scalar(look_bias[:, b, t:t + 1], top[:, b, t:t + 1], temp_sb[:, b, t:t + 1], -1.0,
-                                    op0=ALU.mult, op1=ALU.mult)
+            nc.scalar.activation(look_bias[:, b, t:t + 1], top[:, b, t:t + 1], ACT.Copy, scale=minus_temp[:, b, t:t + 1])
 
         def pair_step(i, m0, m1):
             b, t = divmod(i, PACK)
@@ -212,6 +212,7 @@ def tile_list_peptide_run_features_kernel(
         deal_scales(w2_s[:], raw_s[:])
         deal_w2(0)
         deal_w2(1)
+        nc.scalar.activation(minus_temp[:], temp_sb, ACT.Copy, scale=-1.0)
         load_w1(0, 1, "place_w2")
         gather_words(1, 0, BANK)
         gather_words(1, BANK, S)

from contextlib import ExitStack

import concourse.mybir as mybir

K, T, S, PAIRS, H, N = 1024, 2048, 1024, 512, 1024, 1024
FLOPS = 2 * K * H * S * 2 + 2 * H * N * PAIRS

F32 = mybir.dt.float32
BF16 = mybir.dt.bfloat16
I32 = mybir.dt.int32
U32 = mybir.dt.uint32
U16 = mybir.dt.uint16
U8 = mybir.dt.uint8
FP8X4 = mybir.dt.float8_e4m3fn_x4
FP4X4 = mybir.dt.float4_e2m1fn_x4
ACT = mybir.ActivationFunctionType
ALU = mybir.AluOpType
AXIS = mybir.AxisListType

P = 128
PACK = 4
PASS = P * PACK
BANK = 512
HALF = PAIRS // 2
ROW_TILES = H // P
QUADRANTS = 4
RUN = 4

G_AHEAD = 5
LAG = 2
PASS0_FIRST = 2


def tile_list_peptide_run_features_kernel(
    tc, tab_words, tab_scales, offs, pos1, pos2, w1, shift, w2_words, w2_scales,
    temp, anchor, w3_words, w3_scales, out_0, out_1, out_2,
):
    nc = tc.nc
    with ExitStack() as ctx:
        lists = ctx.enter_context(tc.tile_pool(name="lists", bufs=1))
        keep = ctx.enter_context(tc.tile_pool(name="keep", bufs=1))
        ring = ctx.enter_context(tc.tile_pool(name="ring", bufs=2))
        psum = ctx.enter_context(tc.psum_pool(name="psum", bufs=8))

        def held(shape, dtype, name):
            return keep.tile(shape, dtype, name=name, align_bytes=64)

        def shared(shape, dtype, name, place):
            return keep.tile(shape, dtype, name=name, tag=place, align_bytes=64)

        offs_sb = lists.tile([P, S // 16], U16, name="offs_sb")
        pos1_sb = lists.tile([P, PAIRS // 16], U16, name="pos1_sb")
        pos2_sb = lists.tile([P, PAIRS // 16], U16, name="pos2_sb")

        tab_w = [shared([P, T], U32, "tab_w%d" % a, "place_tab%d" % a) for a in range(2)]
        tab_s = shared([P, T], U8, "tab_s", "place_tab_s")
        v_w = [held([P, S], U32, "v_w%d" % a) for a in range(2)]
        v_s = [held([P, S], U8, "v_s%d" % a) for a in range(2)]
        w2_raw = shared([P, 2 * 2 * H], U8, "w2_raw", "place_w2")
        w2_w = [held([P, 2 * 2 * PASS], U8, "w2_w%d" % b) for b in range(2)]
        raw_s = held([P, 2 * H], U8, "raw_s")
        w2_s = held([P, 2 * H], U8, "w2_s")
        w1_w = [[held([P, PASS], U32, "w1_w%d%d" % (a, b)) for b in range(2)] for a in range(2)]
        w1_s = [[held([P, PASS], U8, "w1_s%d%d" % (a, b)) for b in range(2)] for a in range(2)]
        w3_w = [held([P, N], U32, "w3_w%d" % b) for b in range(2)]
        w3_s = held([P, N], U8, "w3_s")
        look_bias = held([P, 2, PACK], F32, "look_bias")
        minus_temp = held([P, 2, PACK], F32, "minus_temp")
        g_sb = [held([P, S], F32, "g%d" % i) for i in range(ROW_TILES)]
        f_w = [held([P, PAIRS], U32, "f_w%d" % b) for b in range(2)]
        f_s = [held([P, PAIRS], U8, "f_s%d" % b) for b in range(2)]
        y_w = [held([P, PAIRS], U32, "y_w%d" % g) for g in range(2)]
        y_s = held([P, 2, PAIRS], U8, "y_s")
        w1_raw, w1_bf, h_sb, prod, f_bf, y_sb, y_bf = {}, {}, {}, {}, {}, {}, {}

        nc.gpsimd.memset(tab_s[:].bitcast(I32), 0)
        nc.vector.memset(raw_s[:].bitcast(I32), 0)
        nc.gpsimd.memset(v_s[1][:].bitcast(I32), 0)
        nc.sync.dma_start(offs_sb[:], offs)
        nc.sync.dma_start(pos1_sb[:], pos1)
        nc.sync.dma_start(pos2_sb[:], pos2)
        for q in range(QUADRANTS):
            nc.sync.dma_start(tab_s[32 * q:32 * q + 8, :].bitcast(I32), tab_scales[:, 4 * q:4 * q + 4, :].bitcast(I32))

        def load_table(a):
            nc.sync.dma_start(tab_w[a][:].bitcast(I32), tab_words[a].rearrange("p n t -> p (n t)").bitcast(I32))

        def load_w1(a, b, place):
            w1_raw[a, b] = shared([P, PACK, PASS], F32, "w1_raw%d%d" % (a, b), place)
            part = w1[PASS * a:PASS * (a + 1), PASS * b:PASS * (b + 1)]
            nc.sync.dma_start(w1_raw[a, b][:], part.rearrange("(p j) c -> p j c", j=PACK))

        load_table(0)
        nc.sync.dma_start(w2_raw[:].bitcast(I32).rearrange("p (a c) -> p a c", a=2),
                          w2_words.bitcast(I32).rearrange("a p c -> p a c"))
        for q in range(QUADRANTS):
            nc.sync.dma_start(
                raw_s[32 * q:32 * q + 4, :].bitcast(I32).rearrange("r (a c) -> r a c", a=2),
                w2_scales[:, 4 * q:4 * q + 4, :].bitcast(I32).rearrange("a r c -> r a c"))
        load_table(1)
        row_values = held([P, 2, 2, PACK], F32, "row_values")
        for which, values in enumerate((shift, temp)):
            nc.sync.dma_start(row_values[:, which], values.rearrange("(b p t) -> p b t", b=2, t=PACK))
        shift_sb, temp_sb = row_values[:, 0], row_values[:, 1]

        def gather_words(a, j0, j1):
            nc.vector.tensor_copy(v_w[a][:, j0:j1], tab_w[a][:].indirect(offs_sb[:, j0 // 16:j1 // 16]))

        def deal_scales(dst, src):
            nc.vector.tensor_copy(dst.rearrange("p (x t m) -> p x t m", t=PACK, m=P),
                                  src.rearrange("p (x m t) -> p x t m", t=PACK, m=P))

        def deal_w2(b):
            src = w2_raw[:].bitcast(U16).rearrange("p (a b m t) -> p b a t m", a=2, b=2, t=PACK)[:, b]
            dst = w2_w[b][:].bitcast(U16).rearrange("p (a t m) -> p a t m", a=2, t=PACK)
            nc.scalar.copy(dst, src)

        def round_w1(a, b):
            w1_bf[a, b] = ring.tile([P, PACK * PASS], BF16, name="w1_bf", align_bytes=64)
            nc.vector.tensor_copy(w1_bf[a, b][:].rearrange("p (u e m j) -> p u m j e", u=2, e=2, j=PACK),
                                  w1_raw[a, b][:].rearrange("p j (m u e) -> p u m j e", u=2, e=2))

        def quantise_w1(a, b):
            nc.vector.quantize_mx(out=w1_w[a][b][:].bitcast(FP8X4), scales=w1_s[a][b][:], in_=w1_bf[a, b][:])

        def g_step(i, c):
            b, t = divmod(i, PACK)
            cols = slice(BANK * c, BANK * (c + 1))
            acc = psum.tile([P, BANK], F32, name="acc")
            passes = (0, 1) if (c == 0 and i < PASS0_FIRST) else (1, 0)
            for a in passes:
                word0 = PASS * a + P * t
                scale0 = H * a + PASS * b + P * t
                nc.tensor.matmul_mx(
                    out=acc[:],
                    lhsT=w2_w[b][:, 2 * word0:2 * (word0 + P)].bitcast(FP4X4),
                    lhsT_scale=w2_s[:, scale0:scale0 + P],
                    rhs=v_w[a][:, cols].bitcast(FP8X4),
                    rhs_scale=v_s[a][:, cols],
                    start=(a == passes[0]), stop=(a == passes[1]))
            nc.scalar.copy(g_sb[i][:, cols], acc[:])

        def h_step(i, top):
            b, t = divmod(i, PACK)
            h_sb[i] = ring.tile([P, S], F32, name="h_sb", bufs=6)
            for c in range(2):
                cols = slice(BANK * c, BANK * (c + 1))
                acc = psum.tile([P, BANK], F32, name="acc")
                for a in range(2):
                    nc.tensor.matmul_mx(
                        out=acc[:],
                        lhsT=w1_w[a][b][:, P * t:P * (t + 1)].bitcast(FP8X4),
                        lhsT_scale=w1_s[a][b][:, P * t:P * (t + 1)],
                        rhs=v_w[a][:, cols].bitcast(FP8X4),
                        rhs_scale=v_s[0][4 * a:, cols],
                        start=(a == 0), stop=(a == 1))
                nc.scalar.activation(h_sb[i][:, cols], acc[:], ACT.Tanh, bias=shift_sb[:, b, t:t + 1])
            nc.vector.reduce_max(top[:, b, t:t + 1], h_sb[i][:], axis=AXIS.X)
            nc.scalar.activation(look_bias[:, b, t:t + 1], top[:, b, t:t + 1], ACT.Copy, scale=minus_temp[:, b, t:t + 1])

        def pair_step(i, m0, m1):
            b, t = divmod(i, PACK)
            if b not in prod:
                prod[b] = ring.tile([P, PACK, PAIRS], F32, name="prod")
            entries = slice(m0 // 16, m1 // 16)
            look = ring.tile([P, m1 - m0], F32, name="look", bufs=3)
            nc.scalar.activation(look[:], h_sb[i][:].indirect(pos1_sb[:, entries]), ACT.Exp,
                                 bias=look_bias[:, b, t:t + 1], scale=temp_sb[:, b, t:t + 1])
            nc.vector.tensor_tensor(prod[b][:, t, m0:m1], g_sb[i][:].indirect(pos2_sb[:, entries]), look[:], ALU.mult)

        def make_f(b, m0, anchor_sb):
            cols = slice(m0, m0 + HALF)
            f_bf[b, m0] = ring.tile([P, PACK * HALF], BF16, name="f_bf", align_bytes=64)
            nc.vector.tensor_tensor(
                f_bf[b, m0][:].rearrange("p (c i t) -> p c t i", i=RUN, t=PACK),
                prod[b][:, :, cols].rearrange("p t (c i) -> p c t i", i=RUN),
                anchor_sb[:, b].rearrange("p (t c i) -> p c t i", t=PACK, i=RUN)[:, m0 // RUN:(m0 + HALF) // RUN],
                ALU.add)
            nc.vector.quantize_mx(out=f_w[b][:, cols].bitcast(FP8X4), scales=f_s[b][:, cols], in_=f_bf[b, m0][:])

        def y_step(g, m0):
            cols = slice(m0, m0 + HALF)
            y_sb[g, m0] = ring.tile([P, PACK, HALF], F32, name="y_sb", bufs=4)
            for t0 in range(0, PACK, 2):
                acc = psum.tile([P, 2, HALF], F32, name="acc")
                for b in range(2):
                    for e in range(2):
                        word0 = PASS * g + P * (t0 + e)
                        nc.tensor.matmul_mx(
                            out=acc[:, e, :],
                            lhsT=w3_w[b][:, word0:word0 + P].bitcast(FP8X4),
                            lhsT_scale=w3_s[4 * b:, word0:word0 + P],
                            rhs=f_w[b][:, cols].bitcast(FP8X4),
                            rhs_scale=f_s[b][:, cols],
                            start=(b == 0 and e == 0), stop=(b == 1 and e == 1))
                nc.scalar.copy(y_sb[g, m0][:, t0:t0 + 2, :], acc[:])
            nc.sync.dma_start(out_0[PASS * g:PASS * (g + 1), cols].rearrange("(p t) m -> p t m", t=PACK), y_sb[g, m0][:])

        def make_planes(g, m0):
            cols = slice(m0, m0 + HALF)
            y_bf[g, m0] = ring.tile([P, PACK * HALF], BF16, name="y_bf", align_bytes=64)
            nc.vector.tensor_copy(y_bf[g, m0][:].rearrange("p (c i t) -> p c t i", i=RUN, t=PACK),
                                  y_sb[g, m0][:].rearrange("p t (c i) -> p c t i", i=RUN))
            nc.vector.quantize_mx(out=y_w[g][:, cols].bitcast(FP8X4), scales=y_s[:, g, cols], in_=y_bf[g, m0][:])

        nc.vector.tensor_copy(v_s[0][:], tab_s[:].indirect(offs_sb[:]))
        for q in range(QUADRANTS):
            nc.sync.dma_start(v_s[1][32 * q:32 * q + 4, :].bitcast(I32), v_s[0][32 * q + 4:32 * q + 8, :].bitcast(I32))
        load_w1(0, 0, "place_tab_s")
        gather_words(0, 0, S)
        load_w1(1, 0, "place_tab0")
        deal_scales(w2_s[:], raw_s[:])
        deal_w2(0)
        deal_w2(1)
        nc.scalar.activation(minus_temp[:], temp_sb, ACT.Copy, scale=-1.0)
        load_w1(0, 1, "place_w2")
        gather_words(1, 0, BANK)
        gather_words(1, BANK, S)
        load_w1(1, 1, "place_tab1")
        for q in range(QUADRANTS):
            nc.sync.dma_start(raw_s[32 * q:32 * q + 8, 0:N].bitcast(I32), w3_scales[:, 4 * q:4 * q + 4, :].bitcast(I32))
        for a in range(2):
            round_w1(a, 0)
            quantise_w1(a, 0)
        w3_raw = shared([P, 2 * N], U32, "w3_raw", "place_tab0")
        nc.sync.dma_start(w3_raw[:].bitcast(I32).rearrange("p (b c) -> p b c", b=2),
                          w3_words.rearrange("b p n t -> p b (n t)").bitcast(I32))
        round_w1(0, 1)
        quantise_w1(0, 1)
        anchor_sb = shared([P, 2, PACK * PAIRS], F32, "anchor_sb", "place_w2")
        nc.sync.dma_start(anchor_sb[:], anchor.rearrange("(b p t) m -> p b (t m)", b=2, t=PACK))
        round_w1(1, 1)
        quantise_w1(1, 1)

        for c in range(2):
            for i in range(G_AHEAD):
                g_step(i, c)
        top = shared([P, 2, PACK], F32, "top", "place_tab1")
        for i in range(ROW_TILES):
            h_step(i, top)
            behind = i - LAG
            if behind >= G_AHEAD:
                for c in range(2):
                    g_step(behind, c)
            if behind >= 0:
                pair_step(behind, 0, PAIRS)
            if i == PACK - 1:
                deal_scales(w3_s[:], raw_s[:, 0:N])
            if behind >= PACK:
                make_f(0, HALF * (behind - PACK), anchor_sb)

        last = range(ROW_TILES - LAG, ROW_TILES)
        for i in last:
            for c in range(2):
                g_step(i, c)
        for i in last:
            pair_step(i, 0, HALF)
        for b in range(2):
            nc.scalar.copy(w3_w[b][:].rearrange("p (g t m) -> p g m t", g=2, t=PACK),
                           w3_raw[:, N * b:N * (b + 1)].rearrange("p (g m t) -> p g m t", g=2, t=PACK))
        make_f(1, 0, anchor_sb)
        for i in last:
            pair_step(i, HALF, PAIRS)
        y_step(0, 0)
        make_f(1, HALF, anchor_sb)
        pieces = [(g, m0) for m0 in (0, HALF) for g in range(2)]
        for g, m0 in pieces[1:]:
            y_step(g, m0)
        for g, m0 in pieces:
            make_planes(g, m0)

        for g in range(2):
            nc.sync.dma_start(out_1[g].rearrange("p m t -> p (m t)").bitcast(I32), y_w[g][:].bitcast(I32))
        for q in range(QUADRANTS):
            nc.scalar.dma_start(out_2[:, 4 * q:4 * q + 4, :].bitcast(I32).rearrange("g r m -> r g m"),
                                y_s[32 * q:32 * q + 4, :, :].bitcast(I32))
